import numpy as np
import ml_dtypes


def mxq(x, axis, fmt="e4m3"):
    dtype, down = {"e4m3": (ml_dtypes.float8_e4m3fn, 7), "e5m2": (ml_dtypes.float8_e5m2, 14)}[fmt]
    v = np.moveaxis(np.asarray(x, np.float32).astype(ml_dtypes.bfloat16).astype(np.float64), axis, -1)
    blocks = v.reshape(v.shape[:-1] + (-1, 32))
    amax = np.abs(blocks).max(-1, keepdims=True)
    byte = np.maximum(np.where(amax > 0, np.frexp(amax)[1] - 1 + 127, 0) - down, 1)
    scale = np.exp2(byte - 127.0)
    codes = (blocks / scale).astype(np.float32).astype(dtype).astype(np.float64)
    return np.moveaxis((codes * scale).reshape(v.shape), -1, axis)


WIDE = False


def mx_kscale(k):
    if not WIDE:
        return np.ones(k)
    levels = np.array([30, -30])
    if k % 512:
        return np.exp2(np.random.permutation(np.resize(levels, k // 32))).repeat(32)
    a = np.empty((k // 512, 16))
    for p in range(k // 512):
        a[p, :8] = np.random.permutation(np.resize(levels, 8))
        for g in range(8):
            far = levels[np.abs(levels - a[p, g]) >= 10]
            a[p, g + 8] = far[np.random.randint(len(far))]
    return np.exp2(a.ravel()).repeat(32)


def f64(x):
    return np.asarray(x).astype(np.float64)


def striped(idx):
    return np.tile(np.asarray(idx).reshape(-1, 16).T, (8, 1)).astype(np.uint16)


def unstriped(offs):
    return offs[:16].T.reshape(-1).astype(np.int64)


E2M1 = np.array([0.0, 0.5, 1.0, 1.5, 2.0, 3.0, 4.0, 6.0, -0.0, -0.5, -1.0, -1.5, -2.0, -3.0, -4.0, -6.0])


def pack_weight(w, fmt):
    k, n = w.shape
    w = f64(np.asarray(w, np.float32).astype(ml_dtypes.bfloat16)).reshape(k // 32, 32, n)
    amax = np.abs(w).max(1)
    if fmt in ("e4m3", "e5m2"):
        byte = np.frexp(amax)[1] - 1 + 127 - (7 if fmt == "e4m3" else 14)
    else:
        mant, ex = np.frexp(amax / 6.0)
        byte = np.where(mant > 0.5, ex, ex - 1) + 127
    byte = np.clip(np.where(amax > 0, byte, 1), 1, 254)
    scaled = (w * np.exp2(127.0 - byte)[:, None, :]).reshape(k, n).astype(np.float32)
    by_word = np.ascontiguousarray(scaled.reshape(k // 512, 128, 4, n).transpose(0, 1, 3, 2))
    if fmt in ("e4m3", "e5m2"):
        words = by_word.astype(ml_dtypes.float8_e4m3fn if fmt == "e4m3" else ml_dtypes.float8_e5m2).view(np.uint8)
    else:
        c = by_word.astype(ml_dtypes.float4_e2m1fn).view(np.uint8) & 0xF
        words = (c[..., 0::2] | (c[..., 1::2] << 4)).reshape(k // 512, 128, 2 * n)
    return np.ascontiguousarray(words), np.ascontiguousarray(byte.astype(np.uint8).reshape(k // 512, 16, n))


def unpack_weight(words, scales, fmt):
    g, _, n = scales.shape
    words = np.ascontiguousarray(words).reshape(g, 128, n, -1)
    if fmt in ("e4m3", "e5m2"):
        vals = words.view(ml_dtypes.float8_e4m3fn if fmt == "e4m3" else ml_dtypes.float8_e5m2).astype(np.float64)
    else:
        nib = np.empty((g, 128, n, 4), np.uint8)
        nib[..., 0::2] = words & 0xF
        nib[..., 1::2] = words >> 4
        vals = E2M1[nib]
    vals = vals * np.repeat(np.exp2(scales.astype(np.float64) - 127.0), 8, axis=1)[..., None]
    return vals.transpose(0, 1, 3, 2).reshape(g * 512, n)


K, T, J, R, C, O, N, E = 512, 2048, 256, 512, 512, 256, 256, 1024


def setup_inputs():
    n = np.random.standard_normal
    idx = np.random.permutation(T)[:J]
    idx2 = np.random.permutation(T)[:J]
    idx3 = np.random.permutation(C)[:J]
    idx4 = np.random.permutation(C)[:J]
    idx5 = np.random.permutation(C)[:O]
    idx6 = np.random.permutation(E)[:O]
    fk = mx_kscale(K)
    fr = mx_kscale(R)
    xtp = pack_weight(n((K, T)) / fk[:, None], "e5m2")
    wp = pack_weight(n((K, R)) * 1 / np.sqrt(K) * fk[:, None] * fr, "e2m1")
    wbp = pack_weight(n((R, N)) * 1 / np.sqrt(R) / fr[:, None], "e2m1")
    return {
        "xt_words": xtp[0],
        "xt_scales": xtp[1],
        "w_words": wp[0],
        "w_scales": wp[1],
        "wb_words": wbp[0],
        "wb_scales": wbp[1],
        "offs": striped(idx),
        "offs2": striped(idx2),
        "offs3": striped(idx3),
        "offs4": striped(idx4),
        "offs5": striped(idx5),
        "offs6": striped(idx6),
    }


def reference(xt_words, xt_scales, w_words, w_scales, wb_words, wb_scales, offs, offs2, offs3, offs4, offs5, offs6):
    idx = unstriped(offs)
    idx2 = unstriped(offs2)
    idx3 = unstriped(offs3)
    idx4 = unstriped(offs4)
    idx5 = unstriped(offs5)
    idx6 = unstriped(offs6)
    xtu = unpack_weight(xt_words, xt_scales, "e5m2")
    wu = unpack_weight(w_words, w_scales, "e2m1")
    wbu = unpack_weight(wb_words, wb_scales, "e2m1")
    xtidxg = xtu[:, idx]
    a = wu.T @ xtidxg
    xtidx2g = xtu[:, idx2]
    b = wu.T @ xtidx2g
    pw = np.zeros((R, C))
    pw[:, idx3] = a
    pv = np.zeros((R, C))
    pv[:, idx4] = b
    pg = pw + pv
    hid = pg[:, idx5]
    hidq = mxq(hid, 0, "e4m3")
    p = wbu.T @ hidq
    y = np.zeros((N, E))
    y[:, idx6] = p
    return y

@@ -1,0 +1,140 @@
+from contextlib import ExitStack
+
+import concourse.mybir as mybir
+
+K, T, J, R, C, O, N, E = 512, 2048, 256, 512, 512, 256, 256, 1024
+FLOPS = 2 * K * R * 2 * J + 2 * R * N * O
+P = 128
+F32 = mybir.dt.float32
+BF16 = mybir.dt.bfloat16
+I32 = mybir.dt.int32
+U32 = mybir.dt.uint32
+U16 = mybir.dt.uint16
+U8 = mybir.dt.uint8
+E5M2 = mybir.dt.float8_e5m2_x4
+E4M3 = mybir.dt.float8_e4m3fn_x4
+E2M1 = mybir.dt.float4_e2m1fn_x4
+COPY = mybir.ActivationFunctionType.Copy
+ADD = mybir.AluOpType.add
+
+
+def tile_list_tied_shared_one_scattered_kernel(tc, xt_words, xt_scales, w_words, w_scales, wb_words, wb_scales,
+                                                  offs, offs2, offs3, offs4, offs5, offs6, out):
+    nc = tc.nc
+    with ExitStack() as ctx:
+        keep = ctx.enter_context(tc.tile_pool(name="keep", bufs=1))
+        psum = ctx.enter_context(tc.psum_pool(name="psum", bufs=1))
+
+        def sb(name, shape, dtype):
+            return keep.tile(shape, dtype, name=name, align_bytes=64)
+
+        def load_list(name, src):
+            tile = sb(name, [P, J // 16], U16)
+            nc.sync.dma_start(tile[:], src)
+            return tile
+
+        def load_scale_rows(queue, tile, src, q):
+            queue.dma_start(tile[32 * q:32 * q + 4, :].bitcast(I32), src[0, 4 * q:4 * q + 4, :].bitcast(I32))
+
+        xw = sb("xw", [P, T], U32)
+        xs = sb("xs", [P, T], U8)
+        w_raw = sb("w_raw", [P, R], U16)
+        ws_raw = sb("ws_raw", [P, R], U8)
+        wb = sb("wb", [P, 2 * N], U8)
+        wbs = sb("wbs", [P, N], U8)
+
+        nc.scalar.dma_start(xw[:].bitcast(I32), xt_words[0].rearrange("p n t -> p (n t)").bitcast(I32))
+        nc.vector.memset(xs[:].bitcast(I32), 0)
+        nc.gpsimd.memset(ws_raw[:].bitcast(I32), 0)
+        l1 = load_list("l1", offs)
+        l2 = load_list("l2", offs2)
+        nc.sync.dma_start(w_raw[:].bitcast(I32), w_words[0].bitcast(I32))
+        for q in range(4):
+            load_scale_rows(nc.sync, xs, xt_scales, q)
+        for q in range(2):
+            load_scale_rows(nc.gpsimd, ws_raw, w_scales, q)
+        nc.scalar.dma_start(wb[:].bitcast(I32), wb_words[0].bitcast(I32))
+        for q in range(2, 4):
+            load_scale_rows(nc.sync, ws_raw, w_scales, q)
+        l3 = load_list("l3", offs3)
+        l4 = load_list("l4", offs4)
+        l5 = load_list("l5", offs5)
+        l6 = load_list("l6", offs6)
+        for q in range(4):
+            load_scale_rows(nc.gpsimd, wbs, wb_scales, q)
+
+        pw = [sb("pw%d" % i, [P, C], F32) for i in range(2)]
+        pv = [sb("pv%d" % i, [P, C], F32) for i in range(2)]
+        page = [sb("page%d" % i, [P, E], F32) for i in range(2)]
+        for i in range(2):
+            nc.vector.memset(pw[i][:], 0.0)
+            nc.vector.memset(pv[i][:], 0.0)
+        for i in range(2):
+            nc.gpsimd.memset(page[i][:], 0.0)
+
+        w_dealt = sb("w_dealt", [P, 4, P], U16)
+        ws_dealt = sb("ws_dealt", [P, 4, P], U8)
+        nc.vector.tensor_copy(w_dealt[:], w_raw[:].rearrange("p (m t) -> p t m", t=4))
+        xa_s = sb("xa_s", [P, J], U8)
+        xb_s = sb("xb_s", [P, J], U8)
+        xa_w = sb("xa_w", [P, J], U32)
+        xb_w = sb("xb_w", [P, J], U32)
+        nc.vector.tensor_copy(xa_s[:], xs[:].indirect(l1[:]))
+        nc.vector.tensor_copy(xb_s[:], xs[:].indirect(l2[:]))
+        nc.vector.tensor_copy(ws_dealt[:], ws_raw[:].rearrange("p (m t) -> p t m", t=4))
+        nc.vector.tensor_copy(xa_w[:], xw[:].indirect(l1[:]))
+        nc.vector.tensor_copy(xb_w[:], xw[:].indirect(l2[:]))
+
+        def first_product(name, words, scales, t):
+            acc = psum.tile([P, J], F32, name=name, tag=name)
+            nc.tensor.matmul_mx(out=acc[:], lhsT=w_dealt[:, t, :].bitcast(E2M1), lhsT_scale=ws_dealt[:, t, :],
+                                rhs=words[:].bitcast(E5M2), rhs_scale=scales[:], start=True, stop=True)
+            return acc
+
+        acc_a = [first_product("bank_a%d" % t, xa_w, xa_s, t) for t in range(4)]
+        acc_b = [first_product("bank_b%d" % t, xb_w, xb_s, t) for t in range(4)]
+
+        a_sb = [sb("a%d" % t, [P, J], F32) for t in range(4)]
+        b_sb = [sb("b%d" % t, [P, J], F32) for t in range(4)]
+        pg = [sb("pg%d" % t, [P, C], F32) for t in range(4)]
+        hid = sb("hid", [P, O, 4], BF16)
+
+        def join(t):
+            nc.vector.tensor_tensor(pg[t][:], pw[t % 2][:], pv[t % 2][:], ADD)
+
+        def look(t):
+            nc.vector.tensor_copy(hid[:, :, t], pg[t][:].indirect(l5[:]))
+
+        for t in range(4):
+            nc.scalar.copy(a_sb[t][:], acc_a[t][:])
+            if t == 0:
+                nc.vector.tensor_copy(b_sb[t][:], acc_b[t][:])
+            else:
+                nc.scalar.copy(b_sb[t][:], acc_b[t][:])
+            nc.scalar.activation(pw[t % 2][:].indirect(l3[:]), a_sb[t][:], COPY)
+            if t < 3:
+                nc.vector.tensor_copy(pv[t % 2][:].indirect(l4[:]), b_sb[t][:])
+            else:
+                nc.scalar.activation(pv[t % 2][:].indirect(l4[:]), b_sb[t][:], COPY)
+            if t > 0:
+                look(t - 1)
+            join(t)
+        look(3)
+
+        hq = sb("hq", [P, O], U32)
+        hs = sb("hs", [P, O], U8)
+        nc.vector.quantize_mx(out=hq[:].bitcast(E4M3), scales=hs[:], in_=hid[:].rearrange("p o t -> p (o t)"))
+        for i in range(2):
+            acc = psum.tile([P, O], F32, name="second%d" % i, tag="bank_a%d" % i)
+            nc.tensor.matmul_mx(out=acc[:], lhsT=wb[:, 2 * P * i:2 * P * (i + 1)].bitcast(E2M1),
+                                lhsT_scale=wbs[:, P * i:P * (i + 1)], rhs=hq[:].bitcast(E4M3), rhs_scale=hs[:],
+                                start=True, stop=True)
+            p_sb = sb("p%d" % i, [P, O], F32)
+            if i == 0:
+                nc.scalar.copy(p_sb[:], acc[:])
+                nc.scalar.activation(page[i][:].indirect(l6[:]), p_sb[:], COPY)
+                nc.scalar.dma_start(out[P * i:P * (i + 1), :], page[i][:])
+            else:
+                nc.vector.tensor_copy(p_sb[:], acc[:])
+                nc.vector.tensor_copy(page[i][:].indirect(l6[:]), p_sb[:])
+                nc.sync.dma_start(out[P * i:P * (i + 1), :], page[i][:])

@@ -40,92 +40,90 @@ def tile_list_tied_shared_one_scattered_kernel(tc, xt_words, xt_scales, w_words,
         xs = sb("xs", [P, T], U8)
         w_raw = sb("w_raw", [P, R], U16)
         ws_raw = sb("ws_raw", [P, R], U8)
-        wb = sb("wb", [P, 2 * N], U8)
-        wbs = sb("wbs", [P, N], U8)
+        pw = [sb("pw%d" % i, [P, C], F32) for i in range(4)]
+        pv = [sb("pv%d" % i, [P, C], F32) for i in range(2)]
 
-        nc.scalar.dma_start(xw[:].bitcast(I32), xt_words[0].rearrange("p n t -> p (n t)").bitcast(I32))
-        nc.vector.memset(xs[:].bitcast(I32), 0)
-        nc.gpsimd.memset(ws_raw[:].bitcast(I32), 0)
         l1 = load_list("l1", offs)
         l2 = load_list("l2", offs2)
-        nc.sync.dma_start(w_raw[:].bitcast(I32), w_words[0].bitcast(I32))
-        for q in range(4):
-            load_scale_rows(nc.sync, xs, xt_scales, q)
-        for q in range(2):
-            load_scale_rows(nc.gpsimd, ws_raw, w_scales, q)
-        nc.scalar.dma_start(wb[:].bitcast(I32), wb_words[0].bitcast(I32))
-        for q in range(2, 4):
-            load_scale_rows(nc.sync, ws_raw, w_scales, q)
         l3 = load_list("l3", offs3)
         l4 = load_list("l4", offs4)
         l5 = load_list("l5", offs5)
         l6 = load_list("l6", offs6)
+        nc.sync.dma_start(w_raw[:].bitcast(I32), w_words[0].bitcast(I32))
+        nc.sync.dma_start(xw[:].bitcast(I32), xt_words[0].rearrange("p n t -> p (n t)").bitcast(I32))
+        nc.vector.memset(pw[0][:], 0.0)
+        nc.vector.memset(pv[0][:], 0.0)
+        nc.vector.memset(ws_raw[:].bitcast(I32), 0)
+        nc.vector.memset(xs[:].bitcast(I32), 0)
+        load_scale_rows(nc.gpsimd, ws_raw, w_scales, 3)
+        for q in range(3):
+            load_scale_rows(nc.scalar, ws_raw, w_scales, q)
         for q in range(4):
-            load_scale_rows(nc.gpsimd, wbs, wb_scales, q)
-
-        pw = [sb("pw%d" % i, [P, C], F32) for i in range(2)]
-        pv = [sb("pv%d" % i, [P, C], F32) for i in range(2)]
-        page = [sb("page%d" % i, [P, E], F32) for i in range(2)]
-        for i in range(2):
-            nc.vector.memset(pw[i][:], 0.0)
-            nc.vector.memset(pv[i][:], 0.0)
-        for i in range(2):
-            nc.gpsimd.memset(page[i][:], 0.0)
+            load_scale_rows(nc.scalar, xs, xt_scales, q)
+        nc.vector.memset(pw[1][:], 0.0)
+        nc.vector.memset(pv[1][:], 0.0)
+        nc.vector.memset(pw[2][:], 0.0)
+        nc.vector.memset(pw[3][:], 0.0)
 
         w_dealt = sb("w_dealt", [P, 4, P], U16)
         ws_dealt = sb("ws_dealt", [P, 4, P], U8)
         nc.vector.tensor_copy(w_dealt[:], w_raw[:].rearrange("p (m t) -> p t m", t=4))
-        xa_s = sb("xa_s", [P, J], U8)
-        xb_s = sb("xb_s", [P, J], U8)
-        xa_w = sb("xa_w", [P, J], U32)
-        xb_w = sb("xb_w", [P, J], U32)
-        nc.vector.tensor_copy(xa_s[:], xs[:].indirect(l1[:]))
-        nc.vector.tensor_copy(xb_s[:], xs[:].indirect(l2[:]))
+        xg_s = sb("xg_s", [P, 2 * J], U8)
+        xg_w = sb("xg_w", [P, 2 * J], U32)
         nc.vector.tensor_copy(ws_dealt[:], ws_raw[:].rearrange("p (m t) -> p t m", t=4))
-        nc.vector.tensor_copy(xa_w[:], xw[:].indirect(l1[:]))
-        nc.vector.tensor_copy(xb_w[:], xw[:].indirect(l2[:]))
+        nc.vector.tensor_copy(xg_s[:, 0:J], xs[:].indirect(l1[:]))
+        nc.vector.tensor_copy(xg_w[:, 0:J], xw[:].indirect(l1[:]))
+        nc.vector.tensor_copy(xg_s[:, J:2 * J], xs[:].indirect(l2[:]))
+        nc.vector.tensor_copy(xg_w[:, J:2 * J], xw[:].indirect(l2[:]))
 
-        def first_product(name, words, scales, t):
-            acc = psum.tile([P, J], F32, name=name, tag=name)
-            nc.tensor.matmul_mx(out=acc[:], lhsT=w_dealt[:, t, :].bitcast(E2M1), lhsT_scale=ws_dealt[:, t, :],
-                                rhs=words[:].bitcast(E5M2), rhs_scale=scales[:], start=True, stop=True)
+        wb = keep.tile([P, 2 * N], U8, name="wb", tag="w_raw", align_bytes=64)
+        wbs = keep.tile([P, N], U8, name="wbs", tag="ws_raw", align_bytes=64)
+        nc.sync.dma_start(wb[:].bitcast(I32), wb_words[0].bitcast(I32))
+        for q in range(4):
+            load_scale_rows(nc.sync, wbs, wb_scales, q)
+        page = [keep.tile([P, E], F32, name="page%d" % i, tag=("xs", "xw")[i], align_bytes=64) for i in range(2)]
+        for i in range(2):
+            nc.gpsimd.memset(page[i][:], 0.0)
+
+        def first_products(name, planes, lo):
+            acc = psum.tile([P, 2, J], F32, name=name, tag=name)
+            for i, t in enumerate(planes):
+                nc.tensor.matmul_mx(out=acc[:, i, :], lhsT=w_dealt[:, t, :].bitcast(E2M1), lhsT_scale=ws_dealt[:, t, :],
+                                    rhs=xg_w[:, lo:lo + J].bitcast(E5M2), rhs_scale=xg_s[:, lo:lo + J],
+                                    start=True, stop=True)
             return acc
 
-        acc_a = [first_product("bank_a%d" % t, xa_w, xa_s, t) for t in range(4)]
-        acc_b = [first_product("bank_b%d" % t, xb_w, xb_s, t) for t in range(4)]
+        acc_a = [first_products("bank_a%d" % h, (2 * h, 2 * h + 1), 0) for h in range(2)]
+        acc_b = [first_products("bank_b%d" % h, (2 * h, 2 * h + 1), J) for h in range(2)]
 
-        a_sb = [sb("a%d" % t, [P, J], F32) for t in range(4)]
-        b_sb = [sb("b%d" % t, [P, J], F32) for t in range(4)]
-        pg = [sb("pg%d" % t, [P, C], F32) for t in range(4)]
+        a_sb = [sb("a%d" % h, [P, 2, J], F32) for h in range(2)]
+        b_sb = [sb("b%d" % h, [P, 2, J], F32) for h in range(2)]
+        pg = [sb("pg%d" % i, [P, C], F32) for i in range(3)]
         hid = sb("hid", [P, O, 4], BF16)
 
-        def join(t):
-            nc.vector.tensor_tensor(pg[t][:], pw[t % 2][:], pv[t % 2][:], ADD)
-
         def look(t):
-            nc.vector.tensor_copy(hid[:, :, t], pg[t][:].indirect(l5[:]))
+            nc.vector.tensor_copy(hid[:, :, t], pg[min(t, 2)][:].indirect(l5[:]))
 
+        for h in range(2):
+            nc.scalar.copy(a_sb[h][:], acc_a[h][:])
+        nc.vector.tensor_copy(pw[0][:].indirect(l3[:]), a_sb[0][:, 0, :])
         for t in range(4):
-            nc.scalar.copy(a_sb[t][:], acc_a[t][:])
-            if t == 0:
-                nc.vector.tensor_copy(b_sb[t][:], acc_b[t][:])
-            else:
-                nc.scalar.copy(b_sb[t][:], acc_b[t][:])
-            nc.scalar.activation(pw[t % 2][:].indirect(l3[:]), a_sb[t][:], COPY)
+            if t % 2 == 0:
+                nc.scalar.copy(b_sb[t // 2][:], acc_b[t // 2][:])
+            nc.scalar.activation(pv[t % 2][:].indirect(l4[:]), b_sb[t // 2][:, t % 2, :], COPY)
             if t < 3:
-                nc.vector.tensor_copy(pv[t % 2][:].indirect(l4[:]), b_sb[t][:])
-            else:
-                nc.scalar.activation(pv[t % 2][:].indirect(l4[:]), b_sb[t][:], COPY)
+                nc.vector.tensor_copy(pw[t + 1][:].indirect(l3[:]), a_sb[(t + 1) // 2][:, (t + 1) % 2, :])
             if t > 0:
                 look(t - 1)
-            join(t)
+            adder = nc.gpsimd if t < 3 else nc.vector
+            adder.tensor_tensor(pg[min(t, 2)][:], pw[t][:], pv[t % 2][:], ADD)
         look(3)
 
         hq = sb("hq", [P, O], U32)
         hs = sb("hs", [P, O], U8)
         nc.vector.quantize_mx(out=hq[:].bitcast(E4M3), scales=hs[:], in_=hid[:].rearrange("p o t -> p (o t)"))
         for i in range(2):
-            acc = psum.tile([P, O], F32, name="second%d" % i, tag="bank_a%d" % i)
+            acc = psum.tile([P, O], F32, name="second%d" % i, tag="second%d" % i)
             nc.tensor.matmul_mx(out=acc[:], lhsT=wb[:, 2 * P * i:2 * P * (i + 1)].bitcast(E2M1),
                                 lhsT_scale=wbs[:, P * i:P * (i + 1)], rhs=hq[:].bitcast(E4M3), rhs_scale=hs[:],
                                 start=True, stop=True)

@@ -40,38 +40,35 @@ def tile_list_tied_shared_one_scattered_kernel(tc, xt_words, xt_scales, w_words,
         xs = sb("xs", [P, T], U8)
         w_raw = sb("w_raw", [P, R], U16)
         ws_raw = sb("ws_raw", [P, R], U8)
-        pw = [sb("pw%d" % i, [P, C], F32) for i in range(4)]
+        pw = [sb("pw%d" % i, [P, C], F32) for i in range(3)]
         pv = [sb("pv%d" % i, [P, C], F32) for i in range(2)]
 
+        nc.scalar.dma_start(w_raw[:].bitcast(I32), w_words[0].bitcast(I32))
         l1 = load_list("l1", offs)
         l2 = load_list("l2", offs2)
         l3 = load_list("l3", offs3)
         l4 = load_list("l4", offs4)
         l5 = load_list("l5", offs5)
         l6 = load_list("l6", offs6)
-        nc.sync.dma_start(w_raw[:].bitcast(I32), w_words[0].bitcast(I32))
         nc.sync.dma_start(xw[:].bitcast(I32), xt_words[0].rearrange("p n t -> p (n t)").bitcast(I32))
-        nc.vector.memset(pw[0][:], 0.0)
-        nc.vector.memset(pv[0][:], 0.0)
-        nc.vector.memset(ws_raw[:].bitcast(I32), 0)
-        nc.vector.memset(xs[:].bitcast(I32), 0)
+        nc.gpsimd.memset(ws_raw[96:128, :].bitcast(I32), 0)
         load_scale_rows(nc.gpsimd, ws_raw, w_scales, 3)
-        for q in range(3):
-            load_scale_rows(nc.scalar, ws_raw, w_scales, q)
+        nc.vector.memset(xs[:].bitcast(I32), 0)
+        nc.vector.memset(ws_raw[0:96, :].bitcast(I32), 0)
         for q in range(4):
             load_scale_rows(nc.scalar, xs, xt_scales, q)
-        nc.vector.memset(pw[1][:], 0.0)
-        nc.vector.memset(pv[1][:], 0.0)
-        nc.vector.memset(pw[2][:], 0.0)
-        nc.vector.memset(pw[3][:], 0.0)
+        for q in range(3):
+            load_scale_rows(nc.scalar, ws_raw, w_scales, q)
+        for tile in (pw[0], pv[0], pw[1], pv[1], pw[2]):
+            nc.gpsimd.memset(tile[:], 0.0)
 
         w_dealt = sb("w_dealt", [P, 4, P], U16)
         ws_dealt = sb("ws_dealt", [P, 4, P], U8)
         nc.vector.tensor_copy(w_dealt[:], w_raw[:].rearrange("p (m t) -> p t m", t=4))
         xg_s = sb("xg_s", [P, 2 * J], U8)
         xg_w = sb("xg_w", [P, 2 * J], U32)
-        nc.vector.tensor_copy(ws_dealt[:], ws_raw[:].rearrange("p (m t) -> p t m", t=4))
         nc.vector.tensor_copy(xg_s[:, 0:J], xs[:].indirect(l1[:]))
+        nc.vector.tensor_copy(ws_dealt[:], ws_raw[:].rearrange("p (m t) -> p t m", t=4))
         nc.vector.tensor_copy(xg_w[:, 0:J], xw[:].indirect(l1[:]))
         nc.vector.tensor_copy(xg_s[:, J:2 * J], xs[:].indirect(l2[:]))
         nc.vector.tensor_copy(xg_w[:, J:2 * J], xw[:].indirect(l2[:]))
@@ -98,11 +95,11 @@ def tile_list_tied_shared_one_scattered_kernel(tc, xt_words, xt_scales, w_words,
 
         a_sb = [sb("a%d" % h, [P, 2, J], F32) for h in range(2)]
         b_sb = [sb("b%d" % h, [P, 2, J], F32) for h in range(2)]
-        pg = [sb("pg%d" % i, [P, C], F32) for i in range(3)]
+        pg = [sb("pg%d" % i, [P, C], F32) for i in range(4)]
         hid = sb("hid", [P, O, 4], BF16)
 
         def look(t):
-            nc.vector.tensor_copy(hid[:, :, t], pg[min(t, 2)][:].indirect(l5[:]))
+            nc.vector.tensor_copy(hid[:, :, t], pg[t][:].indirect(l5[:]))
 
         for h in range(2):
             nc.scalar.copy(a_sb[h][:], acc_a[h][:])
@@ -112,11 +109,12 @@ def tile_list_tied_shared_one_scattered_kernel(tc, xt_words, xt_scales, w_words,
                 nc.scalar.copy(b_sb[t // 2][:], acc_b[t // 2][:])
             nc.scalar.activation(pv[t % 2][:].indirect(l4[:]), b_sb[t // 2][:, t % 2, :], COPY)
             if t < 3:
-                nc.vector.tensor_copy(pw[t + 1][:].indirect(l3[:]), a_sb[(t + 1) // 2][:, (t + 1) % 2, :])
-            if t > 0:
+                nc.vector.tensor_copy(pw[(t + 1) % 3][:].indirect(l3[:]), a_sb[(t + 1) // 2][:, (t + 1) % 2, :])
+            if t in (1, 2):
                 look(t - 1)
-            adder = nc.gpsimd if t < 3 else nc.vector
-            adder.tensor_tensor(pg[min(t, 2)][:], pw[t][:], pv[t % 2][:], ADD)
+            adder = nc.gpsimd if t < 2 else nc.vector
+            adder.tensor_tensor(pg[t][:], pw[t % 3][:], pv[t % 2][:], ADD)
+        look(2)
         look(3)
 
         hq = sb("hq", [P, O], U32)

@@ -36,11 +36,12 @@ def tile_list_tied_shared_one_scattered_kernel(tc, xt_words, xt_scales, w_words,
         def load_scale_rows(queue, tile, src, q):
             queue.dma_start(tile[32 * q:32 * q + 4, :].bitcast(I32), src[0, 4 * q:4 * q + 4, :].bitcast(I32))
 
-        xw = sb("xw", [P, T], U32)
+        reuse = ctx.enter_context(tc.tile_pool(name="reuse", bufs=1))
+        xw = reuse.tile([P, T], U32, name="xw", offset=4 * C)
         xs = sb("xs", [P, T], U8)
         w_raw = sb("w_raw", [P, R], U16)
         ws_raw = sb("ws_raw", [P, R], U8)
-        pw = [sb("pw%d" % i, [P, C], F32) for i in range(3)]
+        pw = [sb("pw%d" % i, [P, C], F32) for i in range(2)]
         pv = [sb("pv%d" % i, [P, C], F32) for i in range(2)]
 
         nc.scalar.dma_start(w_raw[:].bitcast(I32), w_words[0].bitcast(I32))
@@ -59,7 +60,7 @@ def tile_list_tied_shared_one_scattered_kernel(tc, xt_words, xt_scales, w_words,
             load_scale_rows(nc.scalar, xs, xt_scales, q)
         for q in range(3):
             load_scale_rows(nc.scalar, ws_raw, w_scales, q)
-        for tile in (pw[0], pv[0], pw[1], pv[1], pw[2]):
+        for tile in (pw[0], pw[1], pv[0], pv[1]):
             nc.gpsimd.memset(tile[:], 0.0)
 
         w_dealt = sb("w_dealt", [P, 4, P], U16)
@@ -78,22 +79,23 @@ def tile_list_tied_shared_one_scattered_kernel(tc, xt_words, xt_scales, w_words,
         nc.sync.dma_start(wb[:].bitcast(I32), wb_words[0].bitcast(I32))
         for q in range(4):
             load_scale_rows(nc.sync, wbs, wb_scales, q)
-        page = [keep.tile([P, E], F32, name="page%d" % i, tag=("xs", "xw")[i], align_bytes=64) for i in range(2)]
-        for i in range(2):
-            nc.gpsimd.memset(page[i][:], 0.0)
+        pw.append(reuse.tile([P, C], F32, name="pw2", offset=4 * E))
+        page = [reuse.tile([P, E], F32, name="page%d" % i, offset=i * 4 * (E + C)) for i in range(2)]
+        for tile in (pw[2], page[0], page[1]):
+            nc.gpsimd.memset(tile[:], 0.0)
 
         def first_products(name, planes, lo):
-            acc = psum.tile([P, 2, J], F32, name=name, tag=name)
+            acc = psum.tile([P, len(planes), J], F32, name=name, tag=name)
             for i, t in enumerate(planes):
                 nc.tensor.matmul_mx(out=acc[:, i, :], lhsT=w_dealt[:, t, :].bitcast(E2M1), lhsT_scale=ws_dealt[:, t, :],
                                     rhs=xg_w[:, lo:lo + J].bitcast(E5M2), rhs_scale=xg_s[:, lo:lo + J],
                                     start=True, stop=True)
             return acc
 
-        acc_a = [first_products("bank_a%d" % h, (2 * h, 2 * h + 1), 0) for h in range(2)]
+        acc_a = [first_products("bank_a%d" % t, (t,), 0) for t in range(4)]
         acc_b = [first_products("bank_b%d" % h, (2 * h, 2 * h + 1), J) for h in range(2)]
 
-        a_sb = [sb("a%d" % h, [P, 2, J], F32) for h in range(2)]
+        a_sb = [sb("a%d" % t, [P, J], F32) for t in range(4)]
         b_sb = [sb("b%d" % h, [P, 2, J], F32) for h in range(2)]
         pg = [sb("pg%d" % i, [P, C], F32) for i in range(4)]
         hid = sb("hid", [P, O, 4], BF16)
@@ -101,15 +103,15 @@ def tile_list_tied_shared_one_scattered_kernel(tc, xt_words, xt_scales, w_words,
         def look(t):
             nc.vector.tensor_copy(hid[:, :, t], pg[t][:].indirect(l5[:]))
 
-        for h in range(2):
-            nc.scalar.copy(a_sb[h][:], acc_a[h][:])
-        nc.vector.tensor_copy(pw[0][:].indirect(l3[:]), a_sb[0][:, 0, :])
+        for t in range(4):
+            nc.scalar.copy(a_sb[t][:], acc_a[t][:, 0, :])
+        nc.vector.tensor_copy(pw[0][:].indirect(l3[:]), a_sb[0][:])
         for t in range(4):
             if t % 2 == 0:
                 nc.scalar.copy(b_sb[t // 2][:], acc_b[t // 2][:])
             nc.scalar.activation(pv[t % 2][:].indirect(l4[:]), b_sb[t // 2][:, t % 2, :], COPY)
             if t < 3:
-                nc.vector.tensor_copy(pw[(t + 1) % 3][:].indirect(l3[:]), a_sb[(t + 1) // 2][:, (t + 1) % 2, :])
+                nc.vector.tensor_copy(pw[(t + 1) % 3][:].indirect(l3[:]), a_sb[t + 1][:])
             if t in (1, 2):
                 look(t - 1)
             adder = nc.gpsimd if t < 2 else nc.vector

from contextlib import ExitStack

import concourse.mybir as mybir

K, T, J, R, C, O, N, E = 512, 2048, 256, 512, 512, 256, 256, 1024
FLOPS = 2 * K * R * 2 * J + 2 * R * N * O
P = 128
F32 = mybir.dt.float32
BF16 = mybir.dt.bfloat16
I32 = mybir.dt.int32
U32 = mybir.dt.uint32
U16 = mybir.dt.uint16
U8 = mybir.dt.uint8
E5M2 = mybir.dt.float8_e5m2_x4
E4M3 = mybir.dt.float8_e4m3fn_x4
E2M1 = mybir.dt.float4_e2m1fn_x4
COPY = mybir.ActivationFunctionType.Copy
ADD = mybir.AluOpType.add


def tile_list_tied_shared_one_scattered_kernel(tc, xt_words, xt_scales, w_words, w_scales, wb_words, wb_scales,
                                                  offs, offs2, offs3, offs4, offs5, offs6, out):
    nc = tc.nc
    with ExitStack() as ctx:
        keep = ctx.enter_context(tc.tile_pool(name="keep", bufs=1))
        psum = ctx.enter_context(tc.psum_pool(name="psum", bufs=1))

        def sb(name, shape, dtype):
            return keep.tile(shape, dtype, name=name, align_bytes=64)

        def load_list(name, src):
            tile = sb(name, [P, J // 16], U16)
            nc.sync.dma_start(tile[:], src)
            return tile

        def load_scale_rows(queue, tile, src, q):
            queue.dma_start(tile[32 * q:32 * q + 4, :].bitcast(I32), src[0, 4 * q:4 * q + 4, :].bitcast(I32))

        reuse = ctx.enter_context(tc.tile_pool(name="reuse", bufs=1))
        xw = reuse.tile([P, T], U32, name="xw", offset=4 * C)
        xs = sb("xs", [P, T], U8)
        w_raw = sb("w_raw", [P, R], U16)
        ws_raw = sb("ws_raw", [P, R], U8)
        pw = [sb("pw%d" % i, [P, C], F32) for i in range(2)]
        pv = [sb("pv%d" % i, [P, C], F32) for i in range(2)]

        nc.scalar.dma_start(w_raw[:].bitcast(I32), w_words[0].bitcast(I32))
        l1 = load_list("l1", offs)
        l2 = load_list("l2", offs2)
        l3 = load_list("l3", offs3)
        l4 = load_list("l4", offs4)
        l5 = load_list("l5", offs5)
        l6 = load_list("l6", offs6)
        nc.sync.dma_start(xw[:].bitcast(I32), xt_words[0].rearrange("p n t -> p (n t)").bitcast(I32))
        nc.gpsimd.memset(ws_raw[96:128, :].bitcast(I32), 0)
        load_scale_rows(nc.gpsimd, ws_raw, w_scales, 3)
        nc.vector.memset(xs[:].bitcast(I32), 0)
        nc.vector.memset(ws_raw[0:96, :].bitcast(I32), 0)
        for q in range(4):
            load_scale_rows(nc.scalar, xs, xt_scales, q)
        for q in range(3):
            load_scale_rows(nc.scalar, ws_raw, w_scales, q)
        for tile in (pw[0], pw[1], pv[0], pv[1]):
            nc.gpsimd.memset(tile[:], 0.0)

        w_dealt = sb("w_dealt", [P, 4, P], U16)
        ws_dealt = sb("ws_dealt", [P, 4, P], U8)
        nc.vector.tensor_copy(w_dealt[:], w_raw[:].rearrange("p (m t) -> p t m", t=4))
        xg_s = sb("xg_s", [P, 2 * J], U8)
        xg_w = sb("xg_w", [P, 2 * J], U32)
        nc.vector.tensor_copy(xg_s[:, 0:J], xs[:].indirect(l1[:]))
        nc.vector.tensor_copy(ws_dealt[:], ws_raw[:].rearrange("p (m t) -> p t m", t=4))
        nc.vector.tensor_copy(xg_w[:, 0:J], xw[:].indirect(l1[:]))
        nc.vector.tensor_copy(xg_s[:, J:2 * J], xs[:].indirect(l2[:]))
        nc.vector.tensor_copy(xg_w[:, J:2 * J], xw[:].indirect(l2[:]))

        wb = keep.tile([P, 2 * N], U8, name="wb", tag="w_raw", align_bytes=64)
        wbs = keep.tile([P, N], U8, name="wbs", tag="ws_raw", align_bytes=64)
        nc.sync.dma_start(wb[:].bitcast(I32), wb_words[0].bitcast(I32))
        for q in range(4):
            load_scale_rows(nc.sync, wbs, wb_scales, q)
        pw.append(reuse.tile([P, C], F32, name="pw2", offset=4 * E))
        page = [reuse.tile([P, E], F32, name="page%d" % i, offset=i * 4 * (E + C)) for i in range(2)]
        for tile in (pw[2], page[0], page[1]):
            nc.gpsimd.memset(tile[:], 0.0)

        def first_products(name, planes, lo):
            acc = psum.tile([P, len(planes), J], F32, name=name, tag=name)
            for i, t in enumerate(planes):
                nc.tensor.matmul_mx(out=acc[:, i, :], lhsT=w_dealt[:, t, :].bitcast(E2M1), lhsT_scale=ws_dealt[:, t, :],
                                    rhs=xg_w[:, lo:lo + J].bitcast(E5M2), rhs_scale=xg_s[:, lo:lo + J],
                                    start=True, stop=True)
            return acc

        acc_a = [first_products("bank_a%d" % t, (t,), 0) for t in range(4)]
        acc_b = [first_products("bank_b%d" % h, (2 * h, 2 * h + 1), J) for h in range(2)]

        a_sb = [sb("a%d" % t, [P, J], F32) for t in range(4)]
        b_sb = [sb("b%d" % h, [P, 2, J], F32) for h in range(2)]
        pg = [sb("pg%d" % i, [P, C], F32) for i in range(4)]
        hid = sb("hid", [P, O, 4], BF16)

        def look(t):
            nc.vector.tensor_copy(hid[:, :, t], pg[t][:].indirect(l5[:]))

        for t in range(4):
            nc.scalar.copy(a_sb[t][:], acc_a[t][:, 0, :])
        nc.vector.tensor_copy(pw[0][:].indirect(l3[:]), a_sb[0][:])
        for t in range(4):
            if t % 2 == 0:
                nc.scalar.copy(b_sb[t // 2][:], acc_b[t // 2][:])
            nc.scalar.activation(pv[t % 2][:].indirect(l4[:]), b_sb[t // 2][:, t % 2, :], COPY)
            if t < 3:
                nc.vector.tensor_copy(pw[(t + 1) % 3][:].indirect(l3[:]), a_sb[t + 1][:])
            if t in (1, 2):
                look(t - 1)
            adder = nc.gpsimd if t < 2 else nc.vector
            adder.tensor_tensor(pg[t][:], pw[t % 3][:], pv[t % 2][:], ADD)
        look(2)
        look(3)

        hq = sb("hq", [P, O], U32)
        hs = sb("hs", [P, O], U8)
        nc.vector.quantize_mx(out=hq[:].bitcast(E4M3), scales=hs[:], in_=hid[:].rearrange("p o t -> p (o t)"))
        for i in range(2):
            acc = psum.tile([P, O], F32, name="second%d" % i, tag="second%d" % i)
            nc.tensor.matmul_mx(out=acc[:], lhsT=wb[:, 2 * P * i:2 * P * (i + 1)].bitcast(E2M1),
                                lhsT_scale=wbs[:, P * i:P * (i + 1)], rhs=hq[:].bitcast(E4M3), rhs_scale=hs[:],
                                start=True, stop=True)
            p_sb = sb("p%d" % i, [P, O], F32)
            if i == 0:
                nc.scalar.copy(p_sb[:], acc[:])
                nc.scalar.activation(page[i][:].indirect(l6[:]), p_sb[:], COPY)
                nc.scalar.dma_start(out[P * i:P * (i + 1), :], page[i][:])
            else:
                nc.vector.tensor_copy(p_sb[:], acc[:])
                nc.vector.tensor_copy(page[i][:].indirect(l6[:]), p_sb[:])
                nc.sync.dma_start(out[P * i:P * (i + 1), :], page[i][:])
